import numpy as np
import ml_dtypes


def mxq(x, axis, fmt="e4m3"):
    dtype, down = {"e4m3": (ml_dtypes.float8_e4m3fn, 7), "e5m2": (ml_dtypes.float8_e5m2, 14)}[fmt]
    v = np.moveaxis(np.asarray(x, np.float32).astype(ml_dtypes.bfloat16).astype(np.float64), axis, -1)
    blocks = v.reshape(v.shape[:-1] + (-1, 32))
    amax = np.abs(blocks).max(-1, keepdims=True)
    byte = np.maximum(np.where(amax > 0, np.frexp(amax)[1] - 1 + 127, 0) - down, 1)
    scale = np.exp2(byte - 127.0)
    codes = (blocks / scale).astype(np.float32).astype(dtype).astype(np.float64)
    return np.moveaxis((codes * scale).reshape(v.shape), -1, axis)


WIDE = False


def mx_kscale(k):
    if not WIDE:
        return np.ones(k)
    levels = np.array([10, -10, 5, -5, 0])
    if k % 512:
        return np.exp2(np.random.permutation(np.resize(levels, k // 32))).repeat(32)
    a = np.empty((k // 512, 16))
    for p in range(k // 512):
        a[p, :8] = np.random.permutation(np.resize(levels, 8))
        for g in range(8):
            far = levels[np.abs(levels - a[p, g]) >= 10]
            a[p, g + 8] = far[np.random.randint(len(far))]
    return np.exp2(a.ravel()).repeat(32)


def f64(x):
    return np.asarray(x).astype(np.float64)


def striped(idx):
    return np.tile(idx.reshape(-1, 16).T, (8, 1)).astype(np.uint16)


def unstriped(offs):
    return offs[:16].T.reshape(-1).astype(np.int64)


E2M1 = np.array([0.0, 0.5, 1.0, 1.5, 2.0, 3.0, 4.0, 6.0, -0.0, -0.5, -1.0, -1.5, -2.0, -3.0, -4.0, -6.0])


def pack_weight(w, fmt):
    k, n = w.shape
    w = f64(np.asarray(w, np.float32).astype(ml_dtypes.bfloat16)).reshape(k // 32, 32, n)
    amax = np.abs(w).max(1)
    if fmt == "e4m3":
        byte = np.frexp(amax)[1] - 1 + 127 - 7
    else:
        mant, ex = np.frexp(amax / 6.0)
        byte = np.where(mant > 0.5, ex, ex - 1) + 127
    byte = np.clip(np.where(amax > 0, byte, 1), 1, 254)
    scaled = (w * np.exp2(127.0 - byte)[:, None, :]).reshape(k, n).astype(np.float32)
    by_word = np.ascontiguousarray(scaled.reshape(k // 512, 128, 4, n).transpose(0, 1, 3, 2))
    if fmt == "e4m3":
        words = by_word.astype(ml_dtypes.float8_e4m3fn).view(np.uint8)
    else:
        c = by_word.astype(ml_dtypes.float4_e2m1fn).view(np.uint8) & 0xF
        words = (c[..., 0::2] | (c[..., 1::2] << 4)).reshape(k // 512, 128, 2 * n)
    return np.ascontiguousarray(words), np.ascontiguousarray(byte.astype(np.uint8).reshape(k // 512, 16, n))


def unpack_weight(words, scales, fmt):
    g, _, n = scales.shape
    words = np.ascontiguousarray(words).reshape(g, 128, n, -1)
    if fmt == "e4m3":
        vals = words.view(ml_dtypes.float8_e4m3fn).astype(np.float64)
    else:
        nib = np.empty((g, 128, n, 4), np.uint8)
        nib[..., 0::2] = words & 0xF
        nib[..., 1::2] = words >> 4
        vals = E2M1[nib]
    vals = vals * np.repeat(np.exp2(scales.astype(np.float64) - 127.0), 8, axis=1)[..., None]
    return vals.transpose(0, 1, 3, 2).reshape(g * 512, n)


def gelu(v):
    return 0.5 * v * (1.0 + np.tanh(np.sqrt(2.0 / np.pi) * (v + 0.044715 * v**3)))


K, T, S, H, N, T2 = 1024, 2048, 512, 1024, 768, 1024

def setup_inputs():
    n = np.random.standard_normal
    s = mx_kscale(K)[:, None]
    u = mx_kscale(H)[:, None]
    tab_words, tab_scales = pack_weight(n((K, T)) * s, "e4m3")
    wb8_words, wb8_scales = pack_weight(0.55 * n((K, H)) / np.sqrt(K) / s, "e4m3")
    wd4_words, wd4_scales = pack_weight(0.7 * n((K, N)) / np.sqrt(K) / s, "e2m1")
    return {
        "tab_words": tab_words, "tab_scales": tab_scales,
        "offs": striped(np.random.permutation(T)[:S]),
        "offs2": striped(np.random.permutation(T)[:S]),
        "offs3": striped(np.random.permutation(T2)[:S]),
        "wa": (1.2 * n((K, H)) / np.sqrt(K) / s).astype(np.float32),
        "ba": (0.5 * n(H)).astype(np.float32),
        "wb8_words": wb8_words, "wb8_scales": wb8_scales,
        "gain": (np.exp(0.3 * n(H)) * u[:, 0]).astype(np.float32),
        "wc": (2.7 * n((H, N)) / np.sqrt(H) / u).astype(np.float32),
        "wd4_words": wd4_words, "wd4_scales": wd4_scales,
        "wgo": np.exp(0.3 * n((128, S))).astype(np.float32),
    }

def reference(tab_words, tab_scales, offs, offs2, offs3, wa, ba, wb8_words, wb8_scales,
              gain, wc, wd4_words, wd4_scales, wgo):
    TW = unpack_weight(tab_words, tab_scales, "e4m3")
    v = TW[:, unstriped(offs)]
    v2 = TW[:, unstriped(offs2)]
    wb = unpack_weight(wb8_words, wb8_scales, "e4m3")
    wd = unpack_weight(wd4_words, wd4_scales, "e2m1")
    offer = np.tanh((mxq(f64(wa), 0, "e4m3").T @ v) + f64(ba)[:, None])
    wish = np.sin(wb.T @ v2)
    z = offer * wish * f64(gain)[:, None]
    both = wd.T @ v + wd.T @ v2
    y = np.maximum(mxq(f64(wc), 0, "e4m3").T @ mxq(z, 0, "e4m3"), both)
    out = np.zeros((N, T2))
    out[:, unstriped(offs3)] = np.tile(f64(wgo), (N // 128, 1)) * y
    return out

@@ -1,0 +1,301 @@
+from contextlib import ExitStack
+
+import concourse.mybir as mybir
+from concourse.masks import make_identity
+
+K, T, S, H, N, T2 = 1024, 2048, 512, 1024, 768, 1024
+FLOPS = 2 * S * (2 * K * H + 2 * K * N + H * N)
+
+F32 = mybir.dt.float32
+BF16 = mybir.dt.bfloat16
+I32 = mybir.dt.int32
+U32 = mybir.dt.uint32
+U16 = mybir.dt.uint16
+U8 = mybir.dt.uint8
+FP8X4 = mybir.dt.float8_e4m3fn_x4
+FP4X4 = mybir.dt.float4_e2m1fn_x4
+ALU = mybir.AluOpType
+ACT = mybir.ActivationFunctionType
+
+P = 128
+PACK = 4
+PASS = P * PACK
+PARTS = 2
+W = S // PARTS
+WC_CHUNKS = ((0, 256), (256, 768))
+SINES = 8
+PAGES_ON_VECTOR = 3
+WA_ON_VECTOR = ((0, 0), (0, 1), (1, 0), (1, 1))
+
+
+def tile_list_swap_card_scores_kernel(
+    tc, tab_words, tab_scales, offs, offs2, offs3, wa, ba, wb8_words, wb8_scales,
+    gain, wc, wd4_words, wd4_scales, wgo, out,
+):
+    nc = tc.nc
+    with ExitStack() as ctx:
+        keep = ctx.enter_context(tc.tile_pool(name="keep", bufs=1))
+        ring = ctx.enter_context(tc.tile_pool(name="ring", bufs=3))
+        stage = ctx.enter_context(tc.tile_pool(name="stage", bufs=2))
+        psum = ctx.enter_context(tc.psum_pool(name="psum", bufs=2))
+
+        def held(name, shape, dtype):
+            return keep.tile(shape, dtype, name=name, align_bytes=64)
+
+        lists = [keep.tile([P, S // 16], U16, name=f"list{l}") for l in range(3)]
+        tabw = [stage.tile([P, T], U32, name=f"tabw{a}", tag="wide", align_bytes=64) for a in range(2)]
+        tabs = held("tabs", [P, T], U8)
+        wbs_raw = held("wbs_raw", [P, H], U8)
+        wds = held("wds", [P, 2 * N], U8)
+        moved = held("moved", [P, 2 * S], U8)
+        pages = [held(f"page{n}", [P, T2], F32) for n in range(N // P)]
+        half = held("half", [P, 8], F32)
+
+        nc.gpsimd.memset(tabs[:].bitcast(I32), 0)
+        nc.vector.memset(wbs_raw[:].bitcast(I32), 0)
+        nc.gpsimd.memset(half[:], 0.5)
+        rows = held("rows", [P, PACK, P], F32)
+        identity = held("identity", [P, P], F32)
+        nc.gpsimd.memset(rows[:], 0.0)
+        make_identity(nc, identity[:])
+        for plane in (wds, moved):
+            nc.gpsimd.memset(plane[:].bitcast(I32), 0)
+
+        wa_raw = {(b, a): held(f"wa_raw{b}{a}", [P, PACK, PASS], F32) for b in range(2) for a in range(2)}
+        wb_raw = [held(f"wb_raw{b}", [P, 2, PASS], U32) for b in range(2)]
+        wd = held("wd", [P, 2, 2 * N], U8)
+        wc_raw = {}
+        wgo_sb = held("wgo_sb", [P, S], F32)
+        rows_raw = held("rows_raw", [4, PASS], F32)
+
+        def load_words(tile, words):
+            nc.sync.dma_start(out=tile[:].bitcast(I32), in_=words.rearrange("p c i -> p (c i)").bitcast(I32))
+
+        def load_packed_planes(tile, scales):
+            for q in range(4):
+                nc.sync.dma_start(out=tile[32 * q : 32 * q + 8, :].bitcast(I32),
+                                  in_=scales[:, 4 * q : 4 * q + 4, :].bitcast(I32))
+
+        def load_wa(b, a):
+            block = wa[PASS * a : PASS * (a + 1), PASS * b : PASS * (b + 1)]
+            nc.sync.dma_start(out=wa_raw[b, a][:], in_=block.rearrange("(p j) c -> p j c", j=PACK))
+
+        def load_wc(c):
+            c0, c1 = WC_CHUNKS[c]
+            for b in range(2):
+                tag = "wide" if c == len(WC_CHUNKS) - 1 else f"wc_raw{c}"
+                wc_raw[b, c] = stage.tile([P, PACK, c1 - c0], F32, name=f"wc_raw{b}{c}", tag=tag, align_bytes=64)
+                block = wc[PASS * b : PASS * (b + 1), c0:c1].rearrange("(u t i) n -> t u i n", t=4, i=4)
+                for t in range(PACK):
+                    nc.sync.dma_start(out=wc_raw[b, c][:, t, :], in_=block[t])
+
+        nc.sync.dma_start(out=rows_raw[0:2, :], in_=gain.rearrange("(b c) -> b c", b=2))
+        nc.sync.dma_start(out=rows_raw[2:4, :], in_=ba.rearrange("(b c) -> b c", b=2))
+        nc.sync.dma_start(lists[1][:], offs2)
+        nc.sync.dma_start(lists[0][:], offs)
+        for c0 in range(0, T, T // 4):
+            load_words(tabw[0][:, c0 : c0 + T // 4], tab_words[0][:, c0 : c0 + T // 4])
+        load_packed_planes(tabs, tab_scales)
+        load_words(tabw[1], tab_words[1])
+        load_packed_planes(wbs_raw, wb8_scales)
+        for b in range(2):
+            words = wb8_words[:, :, PASS * b : PASS * (b + 1), :].rearrange("a p c i -> p a (c i)")
+            nc.sync.dma_start(out=wb_raw[b][:].bitcast(I32), in_=words.bitcast(I32))
+        for b in range(2):
+            for a in range(2):
+                load_wa(b, a)
+        nc.sync.dma_start(out=wd[:].bitcast(I32), in_=wd4_words.rearrange("a p c -> p a c").bitcast(I32))
+        for q in range(4):
+            nc.sync.dma_start(
+                out=wds[32 * q : 32 * q + 4, :].bitcast(I32).rearrange("r (a c) -> r a c", a=2),
+                in_=wd4_scales[:, 4 * q : 4 * q + 4, :].bitcast(I32).rearrange("a r c -> r a c"),
+            )
+        load_wc(0)
+        nc.sync.dma_start(out=wgo_sb[:], in_=wgo)
+        nc.sync.dma_start(lists[2][:], offs3)
+
+        nc.scalar.copy(rows[0:4].rearrange("c t (u i) -> c t u i", i=4),
+                       rows_raw[:].rearrange("c (u t i) -> c t u i", t=4, i=4))
+        turned = psum.tile([P, PACK, P], F32, name="both_bank")
+        for t in range(PACK):
+            nc.tensor.transpose(turned[:, t, :], rows[:, t, :], identity[:])
+        gain_ch = turned[:, :, 0:2].rearrange("p t b -> p b t")
+        ba_ch = held("ba_ch", [P, 2, PACK], F32)
+        flip = held("flip", [P, 2, PACK], F32)
+        flip_ba = held("flip_ba", [P, 2, PACK], F32)
+        minus3 = held("minus3", [P, 2, PACK], F32)
+        four = held("four", [P, 2, PACK], F32)
+        root = held("root", [P, 2 * PACK], F32)
+        nc.scalar.activation(four[:], gain_ch, ACT.Abs, scale=4.0)
+        nc.scalar.activation(flip[:], gain_ch, ACT.Sign, scale=-1.0)
+        nc.scalar.copy(ba_ch[:], turned[:, :, 2:4].rearrange("p t b -> p b t"))
+        nc.scalar.activation(minus3[:], four[:], ACT.Copy, scale=-0.75)
+        nc.gpsimd.tensor_tensor(root[:], four[:].rearrange("p b t -> p (b t)"), half[:], ALU.pow)
+        nc.gpsimd.tensor_tensor(flip_ba[:], ba_ch[:], flip[:], ALU.mult)
+
+        vw = {(l, a): held(f"vw{l}{a}", [P, S], U32) for l in range(2) for a in range(2)}
+        vs = held("vs", [P, 2 * S], U8)
+        for l in (1, 0):
+            nc.vector.tensor_copy(vs[:, S * l : S * (l + 1)], tabs[:].indirect(lists[l][:]))
+            for a in range(2):
+                nc.vector.tensor_copy(vw[l, a][:], tabw[a][:].indirect(lists[l][:]))
+        for c in range(1, len(WC_CHUNKS)):
+            load_wc(c)
+        for q in range(4):
+            nc.gpsimd.dma_start(out=moved[32 * q : 32 * q + 4, :].bitcast(I32),
+                                in_=vs[32 * q + 4 : 32 * q + 8, :].bitcast(I32))
+
+        def quantise(name, grouped, width):
+            codes = held(name + "_codes", [P, width], U32)
+            scales = held(name + "_scales", [P, width], U8)
+            nc.vector.quantize_mx(out=codes[:].bitcast(FP8X4), scales=scales[:], in_=grouped[:])
+            return codes, scales
+
+        wa_q = {}
+
+        def prepare_wa(b, a):
+            grouped = stage.tile([P, PASS * PACK], BF16, name="wa_bf", align_bytes=64)
+            dst = grouped[:].rearrange("p (t u i j) -> p t u j i", t=4, i=4, j=PACK)
+            src = wa_raw[b, a][:].rearrange("p j (u t i) -> p t u j i", t=4, i=4)
+            if (b, a) in WA_ON_VECTOR:
+                nc.vector.tensor_copy(dst, src)
+            else:
+                nc.scalar.copy(dst, src)
+            wa_q[b, a] = quantise(f"wa{b}{a}", grouped, PASS)
+
+        wbs = held("wbs", [P, H], U8)
+        nc.scalar.copy(
+            wbs[:].bitcast(U32).rearrange("p (b t u) -> p b t u", b=2, t=4),
+            wbs_raw[:].bitcast(U32).rearrange("p (b u t) -> p b t u", b=2, t=4),
+        )
+        wb = {}
+        for b in range(2):
+            for a in range(2):
+                wb[b, a] = held(f"wb{b}{a}", [P, PASS], U32)
+                nc.scalar.copy(
+                    wb[b, a][:].rearrange("p (t u i) -> p t u i", t=4, i=4),
+                    wb_raw[b][:, a, :].rearrange("p (u t i) -> p t u i", t=4, i=4),
+                )
+        for b in range(2):
+            for a in range(2):
+                prepare_wa(b, a)
+
+        cubic = [held(f"cubic{b}", [P, PACK, S], F32) for b in range(2)]
+
+        def wish_side(b, t):
+            bank = psum.tile([P, S], F32, name="wish_bank")
+            for a in range(2):
+                nc.tensor.matmul_mx(
+                    out=bank[:],
+                    lhsT=wb[b, a][:, P * t : P * (t + 1)].bitcast(FP8X4),
+                    lhsT_scale=wbs[4 * a : P, PASS * b + P * t : PASS * b + P * (t + 1)],
+                    rhs=vw[1, a][:].bitcast(FP8X4), rhs_scale=vs[4 * a : P, S : 2 * S],
+                    start=(a == 0), stop=(a == 1),
+                )
+            sine = ring.tile([P, S], F32, name="sine", bufs=SINES)
+            square = ring.tile([P, S], F32, name="square")
+            nc.scalar.activation(sine[:], bank[:], ACT.Sin, scale=1.0 / 3.0)
+            nc.scalar.activation(square[:], sine[:], ACT.Square, scale=root[:, 4 * b + t : 4 * b + t + 1])
+            nc.vector.scalar_tensor_tensor(
+                cubic[b][:, t, :], square[:], minus3[:, b, t : t + 1], sine[:], ALU.add, ALU.mult)
+
+        def features(b, h):
+            cols = slice(W * h, W * (h + 1))
+            offer = stage.tile([P, PACK, W], F32, name="offer")
+            per_bank = PASS // W
+            for t0 in range(0, PACK, per_bank):
+                bank = psum.tile([P, per_bank, W], F32, name="offer_bank")
+                for k in range(per_bank):
+                    t = t0 + k
+                    for a in range(2):
+                        nc.tensor.matmul_mx(
+                            out=bank[:, k, :],
+                            lhsT=wa_q[b, a][0][:, P * t : P * (t + 1)].bitcast(FP8X4),
+                            lhsT_scale=wa_q[b, a][1][:, P * t : P * (t + 1)],
+                            rhs=vw[0, a][:, cols].bitcast(FP8X4), rhs_scale=vs[4 * a : P, cols],
+                            start=(a == 0), stop=(a == 1),
+                        )
+                for k in range(per_bank):
+                    t = t0 + k
+                    nc.scalar.activation(offer[:, t, :], bank[:, k, :], ACT.Tanh,
+                                         bias=flip_ba[:, b, t : t + 1], scale=flip[:, b, t : t + 1])
+            z = stage.tile([P, W * PACK], BF16, name="z", align_bytes=64)
+            nc.vector.tensor_tensor(
+                z[:].rearrange("p (c i t) -> p c t i", i=2, t=PACK),
+                cubic[b][:, :, cols].rearrange("p t (c i) -> p c t i", i=2),
+                offer[:].rearrange("p t (c i) -> p c t i", i=2),
+                ALU.mult,
+            )
+            return quantise(f"z{b}{h}", z, W)
+
+        for b in range(2):
+            for t in range(PACK):
+                wish_side(b, t)
+
+        wc_q = {}
+
+        def prepare_wc(c):
+            width = WC_CHUNKS[c][1] - WC_CHUNKS[c][0]
+            for b in range(2):
+                grouped = held(f"wc_bf{b}{c}", [P, width * PACK], BF16)
+                nc.scalar.copy(
+                    grouped[:].rearrange("p (c i t) -> p c t i", i=2, t=PACK),
+                    wc_raw[b, c][:].rearrange("p t (c i) -> p c t i", i=2),
+                )
+                wc_q[b, c] = quantise(f"wc{b}{c}", grouped, width)
+
+        both = [held(f"both{n}", [P, S], F32) for n in range(N // P)]
+
+        def both_ends(n):
+            bank = psum.tile([P, S], F32, name="both_bank")
+            passes = [(l, a) for a in range(2) for l in range(2)]
+            for k, (l, a) in enumerate(passes):
+                plane = vs if a == 0 else moved
+                nc.tensor.matmul_mx(
+                    out=bank[:],
+                    lhsT=wd[:, a, 2 * P * n : 2 * P * (n + 1)].bitcast(FP4X4),
+                    lhsT_scale=wds[:, N * a + P * n : N * a + P * (n + 1)],
+                    rhs=vw[l, a][:].bitcast(FP8X4), rhs_scale=plane[:, S * l : S * (l + 1)],
+                    start=(k == 0), stop=(k == len(passes) - 1),
+                )
+            nc.scalar.copy(both[n][:], bank[:])
+
+        def larger_score(n, h, z_q):
+            c = [P * n < c1 for c0, c1 in WC_CHUNKS].index(True)
+            cols = slice(P * n - WC_CHUNKS[c][0], P * (n + 1) - WC_CHUNKS[c][0])
+            bank = psum.tile([P, W], F32, name="score_bank")
+            for b in range(2):
+                nc.tensor.matmul_mx(
+                    out=bank[:],
+                    lhsT=wc_q[b, c][0][:, cols].bitcast(FP8X4), lhsT_scale=wc_q[b, c][1][:, cols],
+                    rhs=z_q[b][0][:].bitcast(FP8X4), rhs_scale=z_q[b][1][:],
+                    start=(b == 0), stop=(b == 1),
+                )
+            y = ring.tile([P, W], F32, name="y")
+            nc.vector.tensor_tensor(y[:], bank[:], both[n][:, W * h : W * (h + 1)], ALU.max)
+            return y
+
+        def place(n, h, y):
+            entries = lists[2][:, W // 16 * h : W // 16 * (h + 1)]
+            nc.vector.tensor_tensor(pages[n][:].indirect(entries), y[:], wgo_sb[:, W * h : W * (h + 1)], ALU.mult)
+            if h == PARTS - 1:
+                nc.sync.dma_start(out=out[P * n : P * (n + 1), :], in_=pages[n][:])
+
+        for n, page in enumerate(pages):
+            (nc.vector if n < PAGES_ON_VECTOR else nc.gpsimd).memset(page[:].bitcast(I32), 0)
+        z_q = {}
+        pending = None
+        for c, (c0, c1) in enumerate(WC_CHUNKS):
+            for h in range(PARTS):
+                if c == 0:
+                    z_q[h] = [features(b, h) for b in range(2)]
+                if h == 0:
+                    prepare_wc(c)
+                for n in range(c0 // P, c1 // P):
+                    if h == 0:
+                        both_ends(n)
+                    y = larger_score(n, h, z_q[h])
+                    if pending is not None:
+                        place(*pending)
+                    pending = (n, h, y)
+        place(*pending)

@@ -24,7 +24,8 @@ PARTS = 2
 W = S // PARTS
 WC_CHUNKS = ((0, 256), (256, 768))
 SINES = 8
-PAGES_ON_VECTOR = 3
+PAGES = 4
+WC_STEP = 256
 WA_ON_VECTOR = ((0, 0), (0, 1), (1, 0), (1, 1))
 
 
@@ -48,18 +49,18 @@ def tile_list_swap_card_scores_kernel(
         wbs_raw = held("wbs_raw", [P, H], U8)
         wds = held("wds", [P, 2 * N], U8)
         moved = held("moved", [P, 2 * S], U8)
-        pages = [held(f"page{n}", [P, T2], F32) for n in range(N // P)]
-        half = held("half", [P, 8], F32)
+        pages = [held(f"page{n}", [P, T2], F32) for n in range(PAGES)]
 
         nc.gpsimd.memset(tabs[:].bitcast(I32), 0)
         nc.vector.memset(wbs_raw[:].bitcast(I32), 0)
-        nc.gpsimd.memset(half[:], 0.5)
         rows = held("rows", [P, PACK, P], F32)
         identity = held("identity", [P, P], F32)
-        nc.gpsimd.memset(rows[:], 0.0)
+        nc.vector.memset(rows[:], 0.0)
         make_identity(nc, identity[:])
         for plane in (wds, moved):
-            nc.gpsimd.memset(plane[:].bitcast(I32), 0)
+            nc.vector.memset(plane[:].bitcast(I32), 0)
+        for page in pages:
+            nc.vector.memset(page[:].bitcast(I32), 0)
 
         wa_raw = {(b, a): held(f"wa_raw{b}{a}", [P, PACK, PASS], F32) for b in range(2) for a in range(2)}
         wb_raw = [held(f"wb_raw{b}", [P, 2, PASS], U32) for b in range(2)]
@@ -101,18 +102,13 @@ def tile_list_swap_card_scores_kernel(
         for b in range(2):
             words = wb8_words[:, :, PASS * b : PASS * (b + 1), :].rearrange("a p c i -> p a (c i)")
             nc.sync.dma_start(out=wb_raw[b][:].bitcast(I32), in_=words.bitcast(I32))
-        for b in range(2):
-            for a in range(2):
-                load_wa(b, a)
-        nc.sync.dma_start(out=wd[:].bitcast(I32), in_=wd4_words.rearrange("a p c -> p a c").bitcast(I32))
         for q in range(4):
             nc.sync.dma_start(
                 out=wds[32 * q : 32 * q + 4, :].bitcast(I32).rearrange("r (a c) -> r a c", a=2),
                 in_=wd4_scales[:, 4 * q : 4 * q + 4, :].bitcast(I32).rearrange("a r c -> r a c"),
             )
-        load_wc(0)
-        nc.sync.dma_start(out=wgo_sb[:], in_=wgo)
-        nc.sync.dma_start(lists[2][:], offs3)
+        for a in range(2):
+            load_wa(0, a)
 
         nc.scalar.copy(rows[0:4].rearrange("c t (u i) -> c t u i", i=4),
                        rows_raw[:].rearrange("c (u t i) -> c t u i", t=4, i=4))
@@ -130,8 +126,7 @@ def tile_list_swap_card_scores_kernel(
         nc.scalar.activation(flip[:], gain_ch, ACT.Sign, scale=-1.0)
         nc.scalar.copy(ba_ch[:], turned[:, :, 2:4].rearrange("p t b -> p b t"))
         nc.scalar.activation(minus3[:], four[:], ACT.Copy, scale=-0.75)
-        nc.gpsimd.tensor_tensor(root[:], four[:].rearrange("p b t -> p (b t)"), half[:], ALU.pow)
-        nc.gpsimd.tensor_tensor(flip_ba[:], ba_ch[:], flip[:], ALU.mult)
+        nc.scalar.activation(root[:], four[:].rearrange("p b t -> p (b t)"), ACT.Sqrt)
 
         vw = {(l, a): held(f"vw{l}{a}", [P, S], U32) for l in range(2) for a in range(2)}
         vs = held("vs", [P, 2 * S], U8)
@@ -139,11 +134,19 @@ def tile_list_swap_card_scores_kernel(
             nc.vector.tensor_copy(vs[:, S * l : S * (l + 1)], tabs[:].indirect(lists[l][:]))
             for a in range(2):
                 nc.vector.tensor_copy(vw[l, a][:], tabw[a][:].indirect(lists[l][:]))
+        for q in range(4):
+            nc.sync.dma_start(out=moved[32 * q : 32 * q + 4, :].bitcast(I32),
+                              in_=vs[32 * q + 4 : 32 * q + 8, :].bitcast(I32))
+        for a in range(2):
+            load_wa(1, a)
+        nc.sync.dma_start(out=wd[:].bitcast(I32), in_=wd4_words.rearrange("a p c -> p a c").bitcast(I32))
+        load_wc(0)
+        nc.sync.dma_start(out=wgo_sb[:], in_=wgo)
+        nc.sync.dma_start(lists[2][:], offs3)
         for c in range(1, len(WC_CHUNKS)):
             load_wc(c)
-        for q in range(4):
-            nc.gpsimd.dma_start(out=moved[32 * q : 32 * q + 4, :].bitcast(I32),
-                                in_=vs[32 * q + 4 : 32 * q + 8, :].bitcast(I32))
+
+        nc.vector.tensor_tensor(flip_ba[:], ba_ch[:], flip[:], ALU.mult)
 
         def quantise(name, grouped, width):
             codes = held(name + "_codes", [P, width], U32)
@@ -183,7 +186,7 @@ def tile_list_swap_card_scores_kernel(
         cubic = [held(f"cubic{b}", [P, PACK, S], F32) for b in range(2)]
 
         def wish_side(b, t):
-            bank = psum.tile([P, S], F32, name="wish_bank")
+            bank = psum.tile([P, S], F32, name="wish_bank", tag="first", bufs=4)
             for a in range(2):
                 nc.tensor.matmul_mx(
                     out=bank[:],
@@ -204,7 +207,7 @@ def tile_list_swap_card_scores_kernel(
             offer = stage.tile([P, PACK, W], F32, name="offer")
             per_bank = PASS // W
             for t0 in range(0, PACK, per_bank):
-                bank = psum.tile([P, per_bank, W], F32, name="offer_bank")
+                bank = psum.tile([P, per_bank, W], F32, name="offer_bank", tag="first", bufs=4)
                 for k in range(per_bank):
                     t = t0 + k
                     for a in range(2):
@@ -234,15 +237,16 @@ def tile_list_swap_card_scores_kernel(
 
         wc_q = {}
 
-        def prepare_wc(c):
-            width = WC_CHUNKS[c][1] - WC_CHUNKS[c][0]
+        def prepare_wc(n0):
+            c = [n0 < c1 for c0, c1 in WC_CHUNKS].index(True)
+            cols = slice(n0 - WC_CHUNKS[c][0], n0 - WC_CHUNKS[c][0] + WC_STEP)
             for b in range(2):
-                grouped = held(f"wc_bf{b}{c}", [P, width * PACK], BF16)
+                grouped = stage.tile([P, WC_STEP * PACK], BF16, name="wc_bf", bufs=4, align_bytes=64)
                 nc.scalar.copy(
                     grouped[:].rearrange("p (c i t) -> p c t i", i=2, t=PACK),
-                    wc_raw[b, c][:].rearrange("p t (c i) -> p c t i", i=2),
+                    wc_raw[b, c][:, :, cols].rearrange("p t (c i) -> p c t i", i=2),
                 )
-                wc_q[b, c] = quantise(f"wc{b}{c}", grouped, width)
+                wc_q[b, n0 // WC_STEP] = quantise(f"wc{b}{n0}", grouped, WC_STEP)
 
         both = [held(f"both{n}", [P, S], F32) for n in range(N // P)]
 
@@ -260,42 +264,46 @@ def tile_list_swap_card_scores_kernel(
                 )
             nc.scalar.copy(both[n][:], bank[:])
 
-        def larger_score(n, h, z_q):
-            c = [P * n < c1 for c0, c1 in WC_CHUNKS].index(True)
-            cols = slice(P * n - WC_CHUNKS[c][0], P * (n + 1) - WC_CHUNKS[c][0])
-            bank = psum.tile([P, W], F32, name="score_bank")
-            for b in range(2):
-                nc.tensor.matmul_mx(
-                    out=bank[:],
-                    lhsT=wc_q[b, c][0][:, cols].bitcast(FP8X4), lhsT_scale=wc_q[b, c][1][:, cols],
-                    rhs=z_q[b][0][:].bitcast(FP8X4), rhs_scale=z_q[b][1][:],
-                    start=(b == 0), stop=(b == 1),
-                )
-            y = ring.tile([P, W], F32, name="y")
-            nc.vector.tensor_tensor(y[:], bank[:], both[n][:, W * h : W * (h + 1)], ALU.max)
+        z_q = {}
+
+        def larger_score(n, parts):
+            c, first = divmod(P * n, WC_STEP)
+            cols = slice(first, first + P)
+            bank = psum.tile([P, len(parts) * W], F32, name="score_bank")
+            for k, h in enumerate(parts):
+                for b in range(2):
+                    nc.tensor.matmul_mx(
+                        out=bank[:, W * k : W * (k + 1)],
+                        lhsT=wc_q[b, c][0][:, cols].bitcast(FP8X4), lhsT_scale=wc_q[b, c][1][:, cols],
+                        rhs=z_q[b, h][0][:].bitcast(FP8X4), rhs_scale=z_q[b, h][1][:],
+                        start=(b == 0), stop=(b == 1),
+                    )
+            y = ring.tile([P, len(parts) * W], F32, name="y")
+            nc.vector.tensor_tensor(y[:], bank[:], both[n][:, W * parts[0] : W * (parts[-1] + 1)], ALU.max)
             return y
 
-        def place(n, h, y):
-            entries = lists[2][:, W // 16 * h : W // 16 * (h + 1)]
-            nc.vector.tensor_tensor(pages[n][:].indirect(entries), y[:], wgo_sb[:, W * h : W * (h + 1)], ALU.mult)
-            if h == PARTS - 1:
-                nc.sync.dma_start(out=out[P * n : P * (n + 1), :], in_=pages[n][:])
+        def place(n, parts, y):
+            j0, j1 = W * parts[0], W * (parts[-1] + 1)
+            page = pages[n % PAGES]
+            nc.vector.tensor_tensor(page[:].indirect(lists[2][:, j0 // 16 : j1 // 16]), y[:], wgo_sb[:, j0:j1], ALU.mult)
+            if j1 == S:
+                nc.sync.dma_start(out=out[P * n : P * (n + 1), :], in_=page[:])
 
-        for n, page in enumerate(pages):
-            (nc.vector if n < PAGES_ON_VECTOR else nc.gpsimd).memset(page[:].bitcast(I32), 0)
-        z_q = {}
+        early = range(WC_CHUNKS[0][1] // P)
+        steps = [(n, [h]) for h in range(PARTS) for n in early]
+        steps = steps + [(n, list(range(PARTS))) for n in range(len(early), N // P)]
         pending = None
-        for c, (c0, c1) in enumerate(WC_CHUNKS):
-            for h in range(PARTS):
-                if c == 0:
-                    z_q[h] = [features(b, h) for b in range(2)]
-                if h == 0:
-                    prepare_wc(c)
-                for n in range(c0 // P, c1 // P):
-                    if h == 0:
-                        both_ends(n)
-                    y = larger_score(n, h, z_q[h])
-                    if pending is not None:
-                        place(*pending)
-                    pending = (n, h, y)
+        for n, parts in steps:
+            for h in parts:
+                for b in range(2):
+                    if (b, h) not in z_q:
+                        z_q[b, h] = features(b, h)
+            if parts[0] == 0:
+                if P * n % WC_STEP == 0:
+                    prepare_wc(P * n)
+                both_ends(n)
+            y = larger_score(n, parts)
+            if pending is not None:
+                place(*pending)
+            pending = (n, parts, y)
         place(*pending)

@@ -24,7 +24,8 @@ PARTS = 2
 W = S // PARTS
 WC_CHUNKS = ((0, 256), (256, 768))
 SINES = 8
-PAGES = 4
+SQUARES = 8
+PAGES = 3
 WC_STEP = 256
 WA_ON_VECTOR = ((0, 0), (0, 1), (1, 0), (1, 1))
 
@@ -51,14 +52,16 @@ def tile_list_swap_card_scores_kernel(
         moved = held("moved", [P, 2 * S], U8)
         pages = [held(f"page{n}", [P, T2], F32) for n in range(PAGES)]
 
-        nc.gpsimd.memset(tabs[:].bitcast(I32), 0)
-        nc.vector.memset(wbs_raw[:].bitcast(I32), 0)
         rows = held("rows", [P, PACK, P], F32)
         identity = held("identity", [P, P], F32)
-        nc.vector.memset(rows[:], 0.0)
+        half = held("half", [P, 2 * PACK], F32)
+        nc.gpsimd.memset(tabs[:].bitcast(I32), 0)
         make_identity(nc, identity[:])
+        nc.gpsimd.memset(half[:], 0.5)
         for plane in (wds, moved):
-            nc.vector.memset(plane[:].bitcast(I32), 0)
+            nc.gpsimd.memset(plane[:].bitcast(I32), 0)
+        nc.vector.memset(wbs_raw[:].bitcast(I32), 0)
+        nc.vector.memset(rows[:], 0.0)
         for page in pages:
             nc.vector.memset(page[:].bitcast(I32), 0)
 
@@ -77,10 +80,6 @@ def tile_list_swap_card_scores_kernel(
                 nc.sync.dma_start(out=tile[32 * q : 32 * q + 8, :].bitcast(I32),
                                   in_=scales[:, 4 * q : 4 * q + 4, :].bitcast(I32))
 
-        def load_wa(b, a):
-            block = wa[PASS * a : PASS * (a + 1), PASS * b : PASS * (b + 1)]
-            nc.sync.dma_start(out=wa_raw[b, a][:], in_=block.rearrange("(p j) c -> p j c", j=PACK))
-
         def load_wc(c):
             c0, c1 = WC_CHUNKS[c]
             for b in range(2):
@@ -90,15 +89,15 @@ def tile_list_swap_card_scores_kernel(
                 for t in range(PACK):
                     nc.sync.dma_start(out=wc_raw[b, c][:, t, :], in_=block[t])
 
-        nc.sync.dma_start(out=rows_raw[0:2, :], in_=gain.rearrange("(b c) -> b c", b=2))
-        nc.sync.dma_start(out=rows_raw[2:4, :], in_=ba.rearrange("(b c) -> b c", b=2))
         nc.sync.dma_start(lists[1][:], offs2)
         nc.sync.dma_start(lists[0][:], offs)
-        for c0 in range(0, T, T // 4):
-            load_words(tabw[0][:, c0 : c0 + T // 4], tab_words[0][:, c0 : c0 + T // 4])
+        nc.sync.dma_start(out=rows_raw[0:2, :], in_=gain.rearrange("(b c) -> b c", b=2))
+        nc.sync.dma_start(out=rows_raw[2:4, :], in_=ba.rearrange("(b c) -> b c", b=2))
+        load_words(tabw[0], tab_words[0])
         load_packed_planes(tabs, tab_scales)
         load_words(tabw[1], tab_words[1])
         load_packed_planes(wbs_raw, wb8_scales)
+        nc.sync.dma_start(lists[2][:], offs3)
         for b in range(2):
             words = wb8_words[:, :, PASS * b : PASS * (b + 1), :].rearrange("a p c i -> p a (c i)")
             nc.sync.dma_start(out=wb_raw[b][:].bitcast(I32), in_=words.bitcast(I32))
@@ -107,8 +106,13 @@ def tile_list_swap_card_scores_kernel(
                 out=wds[32 * q : 32 * q + 4, :].bitcast(I32).rearrange("r (a c) -> r a c", a=2),
                 in_=wd4_scales[:, 4 * q : 4 * q + 4, :].bitcast(I32).rearrange("a r c -> r a c"),
             )
-        for a in range(2):
-            load_wa(0, a)
+        for b in range(2):
+            for a in range(2):
+                block = wa[PASS * a : PASS * (a + 1), PASS * b : PASS * (b + 1)]
+                nc.sync.dma_start(out=wa_raw[b, a][:], in_=block.rearrange("(p j) c -> p j c", j=PACK))
+        nc.sync.dma_start(out=wd[:].bitcast(I32), in_=wd4_words.rearrange("a p c -> p a c").bitcast(I32))
+        load_wc(0)
+        nc.sync.dma_start(out=wgo_sb[:], in_=wgo)
 
         nc.scalar.copy(rows[0:4].rearrange("c t (u i) -> c t u i", i=4),
                        rows_raw[:].rearrange("c (u t i) -> c t u i", t=4, i=4))
@@ -126,7 +130,9 @@ def tile_list_swap_card_scores_kernel(
         nc.scalar.activation(flip[:], gain_ch, ACT.Sign, scale=-1.0)
         nc.scalar.copy(ba_ch[:], turned[:, :, 2:4].rearrange("p t b -> p b t"))
         nc.scalar.activation(minus3[:], four[:], ACT.Copy, scale=-0.75)
-        nc.scalar.activation(root[:], four[:].rearrange("p b t -> p (b t)"), ACT.Sqrt)
+        nc.gpsimd.tensor_tensor(root[:], four[:].rearrange("p b t -> p (b t)"), half[:], ALU.pow)
+
+        nc.gpsimd.tensor_tensor(flip_ba[:], ba_ch[:], flip[:], ALU.mult)
 
         vw = {(l, a): held(f"vw{l}{a}", [P, S], U32) for l in range(2) for a in range(2)}
         vs = held("vs", [P, 2 * S], U8)
@@ -135,18 +141,11 @@ def tile_list_swap_card_scores_kernel(
             for a in range(2):
                 nc.vector.tensor_copy(vw[l, a][:], tabw[a][:].indirect(lists[l][:]))
         for q in range(4):
-            nc.sync.dma_start(out=moved[32 * q : 32 * q + 4, :].bitcast(I32),
-                              in_=vs[32 * q + 4 : 32 * q + 8, :].bitcast(I32))
-        for a in range(2):
-            load_wa(1, a)
-        nc.sync.dma_start(out=wd[:].bitcast(I32), in_=wd4_words.rearrange("a p c -> p a c").bitcast(I32))
-        load_wc(0)
-        nc.sync.dma_start(out=wgo_sb[:], in_=wgo)
-        nc.sync.dma_start(lists[2][:], offs3)
+            nc.gpsimd.dma_start(out=moved[32 * q : 32 * q + 4, :].bitcast(I32),
+                                in_=vs[32 * q + 4 : 32 * q + 8, :].bitcast(I32))
         for c in range(1, len(WC_CHUNKS)):
             load_wc(c)
 
-        nc.vector.tensor_tensor(flip_ba[:], ba_ch[:], flip[:], ALU.mult)
 
         def quantise(name, grouped, width):
             codes = held(name + "_codes", [P, width], U32)
@@ -179,9 +178,6 @@ def tile_list_swap_card_scores_kernel(
                     wb[b, a][:].rearrange("p (t u i) -> p t u i", t=4, i=4),
                     wb_raw[b][:, a, :].rearrange("p (u t i) -> p t u i", t=4, i=4),
                 )
-        for b in range(2):
-            for a in range(2):
-                prepare_wa(b, a)
 
         cubic = [held(f"cubic{b}", [P, PACK, S], F32) for b in range(2)]
 
@@ -196,7 +192,7 @@ def tile_list_swap_card_scores_kernel(
                     start=(a == 0), stop=(a == 1),
                 )
             sine = ring.tile([P, S], F32, name="sine", bufs=SINES)
-            square = ring.tile([P, S], F32, name="square")
+            square = ring.tile([P, S], F32, name="square", bufs=SQUARES)
             nc.scalar.activation(sine[:], bank[:], ACT.Sin, scale=1.0 / 3.0)
             nc.scalar.activation(square[:], sine[:], ACT.Square, scale=root[:, 4 * b + t : 4 * b + t + 1])
             nc.vector.scalar_tensor_tensor(
@@ -231,6 +227,9 @@ def tile_list_swap_card_scores_kernel(
             )
             return quantise(f"z{b}{h}", z, W)
 
+        for b in range(2):
+            for a in range(2):
+                prepare_wa(b, a)
         for b in range(2):
             for t in range(PACK):
                 wish_side(b, t)

from contextlib import ExitStack

import concourse.mybir as mybir
from concourse.masks import make_identity

K, T, S, H, N, T2 = 1024, 2048, 512, 1024, 768, 1024
FLOPS = 2 * S * (2 * K * H + 2 * K * N + H * N)

F32 = mybir.dt.float32
BF16 = mybir.dt.bfloat16
I32 = mybir.dt.int32
U32 = mybir.dt.uint32
U16 = mybir.dt.uint16
U8 = mybir.dt.uint8
FP8X4 = mybir.dt.float8_e4m3fn_x4
FP4X4 = mybir.dt.float4_e2m1fn_x4
ALU = mybir.AluOpType
ACT = mybir.ActivationFunctionType

P = 128
PACK = 4
PASS = P * PACK
PARTS = 2
W = S // PARTS
WC_CHUNKS = ((0, 256), (256, 768))
SINES = 8
SQUARES = 8
PAGES = 3
WC_STEP = 256
WA_ON_VECTOR = ((0, 0), (0, 1), (1, 0), (1, 1))


def tile_list_swap_card_scores_kernel(
    tc, tab_words, tab_scales, offs, offs2, offs3, wa, ba, wb8_words, wb8_scales,
    gain, wc, wd4_words, wd4_scales, wgo, out,
):
    nc = tc.nc
    with ExitStack() as ctx:
        keep = ctx.enter_context(tc.tile_pool(name="keep", bufs=1))
        ring = ctx.enter_context(tc.tile_pool(name="ring", bufs=3))
        stage = ctx.enter_context(tc.tile_pool(name="stage", bufs=2))
        psum = ctx.enter_context(tc.psum_pool(name="psum", bufs=2))

        def held(name, shape, dtype):
            return keep.tile(shape, dtype, name=name, align_bytes=64)

        lists = [keep.tile([P, S // 16], U16, name=f"list{l}") for l in range(3)]
        tabw = [stage.tile([P, T], U32, name=f"tabw{a}", tag="wide", align_bytes=64) for a in range(2)]
        tabs = held("tabs", [P, T], U8)
        wbs_raw = held("wbs_raw", [P, H], U8)
        wds = held("wds", [P, 2 * N], U8)
        moved = held("moved", [P, 2 * S], U8)
        pages = [held(f"page{n}", [P, T2], F32) for n in range(PAGES)]

        rows = held("rows", [P, PACK, P], F32)
        identity = held("identity", [P, P], F32)
        half = held("half", [P, 2 * PACK], F32)
        nc.gpsimd.memset(tabs[:].bitcast(I32), 0)
        make_identity(nc, identity[:])
        nc.gpsimd.memset(half[:], 0.5)
        for plane in (wds, moved):
            nc.gpsimd.memset(plane[:].bitcast(I32), 0)
        nc.vector.memset(wbs_raw[:].bitcast(I32), 0)
        nc.vector.memset(rows[:], 0.0)
        for page in pages:
            nc.vector.memset(page[:].bitcast(I32), 0)

        wa_raw = {(b, a): held(f"wa_raw{b}{a}", [P, PACK, PASS], F32) for b in range(2) for a in range(2)}
        wb_raw = [held(f"wb_raw{b}", [P, 2, PASS], U32) for b in range(2)]
        wd = held("wd", [P, 2, 2 * N], U8)
        wc_raw = {}
        wgo_sb = held("wgo_sb", [P, S], F32)
        rows_raw = held("rows_raw", [4, PASS], F32)

        def load_words(tile, words):
            nc.sync.dma_start(out=tile[:].bitcast(I32), in_=words.rearrange("p c i -> p (c i)").bitcast(I32))

        def load_packed_planes(tile, scales):
            for q in range(4):
                nc.sync.dma_start(out=tile[32 * q : 32 * q + 8, :].bitcast(I32),
                                  in_=scales[:, 4 * q : 4 * q + 4, :].bitcast(I32))

        def load_wc(c):
            c0, c1 = WC_CHUNKS[c]
            for b in range(2):
                tag = "wide" if c == len(WC_CHUNKS) - 1 else f"wc_raw{c}"
                wc_raw[b, c] = stage.tile([P, PACK, c1 - c0], F32, name=f"wc_raw{b}{c}", tag=tag, align_bytes=64)
                block = wc[PASS * b : PASS * (b + 1), c0:c1].rearrange("(u t i) n -> t u i n", t=4, i=4)
                for t in range(PACK):
                    nc.sync.dma_start(out=wc_raw[b, c][:, t, :], in_=block[t])

        nc.sync.dma_start(lists[1][:], offs2)
        nc.sync.dma_start(lists[0][:], offs)
        nc.sync.dma_start(out=rows_raw[0:2, :], in_=gain.rearrange("(b c) -> b c", b=2))
        nc.sync.dma_start(out=rows_raw[2:4, :], in_=ba.rearrange("(b c) -> b c", b=2))
        load_words(tabw[0], tab_words[0])
        load_packed_planes(tabs, tab_scales)
        load_words(tabw[1], tab_words[1])
        load_packed_planes(wbs_raw, wb8_scales)
        nc.sync.dma_start(lists[2][:], offs3)
        for b in range(2):
            words = wb8_words[:, :, PASS * b : PASS * (b + 1), :].rearrange("a p c i -> p a (c i)")
            nc.sync.dma_start(out=wb_raw[b][:].bitcast(I32), in_=words.bitcast(I32))
        for q in range(4):
            nc.sync.dma_start(
                out=wds[32 * q : 32 * q + 4, :].bitcast(I32).rearrange("r (a c) -> r a c", a=2),
                in_=wd4_scales[:, 4 * q : 4 * q + 4, :].bitcast(I32).rearrange("a r c -> r a c"),
            )
        for b in range(2):
            for a in range(2):
                block = wa[PASS * a : PASS * (a + 1), PASS * b : PASS * (b + 1)]
                nc.sync.dma_start(out=wa_raw[b, a][:], in_=block.rearrange("(p j) c -> p j c", j=PACK))
        nc.sync.dma_start(out=wd[:].bitcast(I32), in_=wd4_words.rearrange("a p c -> p a c").bitcast(I32))
        load_wc(0)
        nc.sync.dma_start(out=wgo_sb[:], in_=wgo)

        nc.scalar.copy(rows[0:4].rearrange("c t (u i) -> c t u i", i=4),
                       rows_raw[:].rearrange("c (u t i) -> c t u i", t=4, i=4))
        turned = psum.tile([P, PACK, P], F32, name="both_bank")
        for t in range(PACK):
            nc.tensor.transpose(turned[:, t, :], rows[:, t, :], identity[:])
        gain_ch = turned[:, :, 0:2].rearrange("p t b -> p b t")
        ba_ch = held("ba_ch", [P, 2, PACK], F32)
        flip = held("flip", [P, 2, PACK], F32)
        flip_ba = held("flip_ba", [P, 2, PACK], F32)
        minus3 = held("minus3", [P, 2, PACK], F32)
        four = held("four", [P, 2, PACK], F32)
        root = held("root", [P, 2 * PACK], F32)
        nc.scalar.activation(four[:], gain_ch, ACT.Abs, scale=4.0)
        nc.scalar.activation(flip[:], gain_ch, ACT.Sign, scale=-1.0)
        nc.scalar.copy(ba_ch[:], turned[:, :, 2:4].rearrange("p t b -> p b t"))
        nc.scalar.activation(minus3[:], four[:], ACT.Copy, scale=-0.75)
        nc.gpsimd.tensor_tensor(root[:], four[:].rearrange("p b t -> p (b t)"), half[:], ALU.pow)

        nc.gpsimd.tensor_tensor(flip_ba[:], ba_ch[:], flip[:], ALU.mult)

        vw = {(l, a): held(f"vw{l}{a}", [P, S], U32) for l in range(2) for a in range(2)}
        vs = held("vs", [P, 2 * S], U8)
        for l in (1, 0):
            nc.vector.tensor_copy(vs[:, S * l : S * (l + 1)], tabs[:].indirect(lists[l][:]))
            for a in range(2):
                nc.vector.tensor_copy(vw[l, a][:], tabw[a][:].indirect(lists[l][:]))
        for q in range(4):
            nc.gpsimd.dma_start(out=moved[32 * q : 32 * q + 4, :].bitcast(I32),
                                in_=vs[32 * q + 4 : 32 * q + 8, :].bitcast(I32))
        for c in range(1, len(WC_CHUNKS)):
            load_wc(c)


        def quantise(name, grouped, width):
            codes = held(name + "_codes", [P, width], U32)
            scales = held(name + "_scales", [P, width], U8)
            nc.vector.quantize_mx(out=codes[:].bitcast(FP8X4), scales=scales[:], in_=grouped[:])
            return codes, scales

        wa_q = {}

        def prepare_wa(b, a):
            grouped = stage.tile([P, PASS * PACK], BF16, name="wa_bf", align_bytes=64)
            dst = grouped[:].rearrange("p (t u i j) -> p t u j i", t=4, i=4, j=PACK)
            src = wa_raw[b, a][:].rearrange("p j (u t i) -> p t u j i", t=4, i=4)
            if (b, a) in WA_ON_VECTOR:
                nc.vector.tensor_copy(dst, src)
            else:
                nc.scalar.copy(dst, src)
            wa_q[b, a] = quantise(f"wa{b}{a}", grouped, PASS)

        wbs = held("wbs", [P, H], U8)
        nc.scalar.copy(
            wbs[:].bitcast(U32).rearrange("p (b t u) -> p b t u", b=2, t=4),
            wbs_raw[:].bitcast(U32).rearrange("p (b u t) -> p b t u", b=2, t=4),
        )
        wb = {}
        for b in range(2):
            for a in range(2):
                wb[b, a] = held(f"wb{b}{a}", [P, PASS], U32)
                nc.scalar.copy(
                    wb[b, a][:].rearrange("p (t u i) -> p t u i", t=4, i=4),
                    wb_raw[b][:, a, :].rearrange("p (u t i) -> p t u i", t=4, i=4),
                )

        cubic = [held(f"cubic{b}", [P, PACK, S], F32) for b in range(2)]

        def wish_side(b, t):
            bank = psum.tile([P, S], F32, name="wish_bank", tag="first", bufs=4)
            for a in range(2):
                nc.tensor.matmul_mx(
                    out=bank[:],
                    lhsT=wb[b, a][:, P * t : P * (t + 1)].bitcast(FP8X4),
                    lhsT_scale=wbs[4 * a : P, PASS * b + P * t : PASS * b + P * (t + 1)],
                    rhs=vw[1, a][:].bitcast(FP8X4), rhs_scale=vs[4 * a : P, S : 2 * S],
                    start=(a == 0), stop=(a == 1),
                )
            sine = ring.tile([P, S], F32, name="sine", bufs=SINES)
            square = ring.tile([P, S], F32, name="square", bufs=SQUARES)
            nc.scalar.activation(sine[:], bank[:], ACT.Sin, scale=1.0 / 3.0)
            nc.scalar.activation(square[:], sine[:], ACT.Square, scale=root[:, 4 * b + t : 4 * b + t + 1])
            nc.vector.scalar_tensor_tensor(
                cubic[b][:, t, :], square[:], minus3[:, b, t : t + 1], sine[:], ALU.add, ALU.mult)

        def features(b, h):
            cols = slice(W * h, W * (h + 1))
            offer = stage.tile([P, PACK, W], F32, name="offer")
            per_bank = PASS // W
            for t0 in range(0, PACK, per_bank):
                bank = psum.tile([P, per_bank, W], F32, name="offer_bank", tag="first", bufs=4)
                for k in range(per_bank):
                    t = t0 + k
                    for a in range(2):
                        nc.tensor.matmul_mx(
                            out=bank[:, k, :],
                            lhsT=wa_q[b, a][0][:, P * t : P * (t + 1)].bitcast(FP8X4),
                            lhsT_scale=wa_q[b, a][1][:, P * t : P * (t + 1)],
                            rhs=vw[0, a][:, cols].bitcast(FP8X4), rhs_scale=vs[4 * a : P, cols],
                            start=(a == 0), stop=(a == 1),
                        )
                for k in range(per_bank):
                    t = t0 + k
                    nc.scalar.activation(offer[:, t, :], bank[:, k, :], ACT.Tanh,
                                         bias=flip_ba[:, b, t : t + 1], scale=flip[:, b, t : t + 1])
            z = stage.tile([P, W * PACK], BF16, name="z", align_bytes=64)
            nc.vector.tensor_tensor(
                z[:].rearrange("p (c i t) -> p c t i", i=2, t=PACK),
                cubic[b][:, :, cols].rearrange("p t (c i) -> p c t i", i=2),
                offer[:].rearrange("p t (c i) -> p c t i", i=2),
                ALU.mult,
            )
            return quantise(f"z{b}{h}", z, W)

        for b in range(2):
            for a in range(2):
                prepare_wa(b, a)
        for b in range(2):
            for t in range(PACK):
                wish_side(b, t)

        wc_q = {}

        def prepare_wc(n0):
            c = [n0 < c1 for c0, c1 in WC_CHUNKS].index(True)
            cols = slice(n0 - WC_CHUNKS[c][0], n0 - WC_CHUNKS[c][0] + WC_STEP)
            for b in range(2):
                grouped = stage.tile([P, WC_STEP * PACK], BF16, name="wc_bf", bufs=4, align_bytes=64)
                nc.scalar.copy(
                    grouped[:].rearrange("p (c i t) -> p c t i", i=2, t=PACK),
                    wc_raw[b, c][:, :, cols].rearrange("p t (c i) -> p c t i", i=2),
                )
                wc_q[b, n0 // WC_STEP] = quantise(f"wc{b}{n0}", grouped, WC_STEP)

        both = [held(f"both{n}", [P, S], F32) for n in range(N // P)]

        def both_ends(n):
            bank = psum.tile([P, S], F32, name="both_bank")
            passes = [(l, a) for a in range(2) for l in range(2)]
            for k, (l, a) in enumerate(passes):
                plane = vs if a == 0 else moved
                nc.tensor.matmul_mx(
                    out=bank[:],
                    lhsT=wd[:, a, 2 * P * n : 2 * P * (n + 1)].bitcast(FP4X4),
                    lhsT_scale=wds[:, N * a + P * n : N * a + P * (n + 1)],
                    rhs=vw[l, a][:].bitcast(FP8X4), rhs_scale=plane[:, S * l : S * (l + 1)],
                    start=(k == 0), stop=(k == len(passes) - 1),
                )
            nc.scalar.copy(both[n][:], bank[:])

        z_q = {}

        def larger_score(n, parts):
            c, first = divmod(P * n, WC_STEP)
            cols = slice(first, first + P)
            bank = psum.tile([P, len(parts) * W], F32, name="score_bank")
            for k, h in enumerate(parts):
                for b in range(2):
                    nc.tensor.matmul_mx(
                        out=bank[:, W * k : W * (k + 1)],
                        lhsT=wc_q[b, c][0][:, cols].bitcast(FP8X4), lhsT_scale=wc_q[b, c][1][:, cols],
                        rhs=z_q[b, h][0][:].bitcast(FP8X4), rhs_scale=z_q[b, h][1][:],
                        start=(b == 0), stop=(b == 1),
                    )
            y = ring.tile([P, len(parts) * W], F32, name="y")
            nc.vector.tensor_tensor(y[:], bank[:], both[n][:, W * parts[0] : W * (parts[-1] + 1)], ALU.max)
            return y

        def place(n, parts, y):
            j0, j1 = W * parts[0], W * (parts[-1] + 1)
            page = pages[n % PAGES]
            nc.vector.tensor_tensor(page[:].indirect(lists[2][:, j0 // 16 : j1 // 16]), y[:], wgo_sb[:, j0:j1], ALU.mult)
            if j1 == S:
                nc.sync.dma_start(out=out[P * n : P * (n + 1), :], in_=page[:])

        early = range(WC_CHUNKS[0][1] // P)
        steps = [(n, [h]) for h in range(PARTS) for n in early]
        steps = steps + [(n, list(range(PARTS))) for n in range(len(early), N // P)]
        pending = None
        for n, parts in steps:
            for h in parts:
                for b in range(2):
                    if (b, h) not in z_q:
                        z_q[b, h] = features(b, h)
            if parts[0] == 0:
                if P * n % WC_STEP == 0:
                    prepare_wc(P * n)
                both_ends(n)
            y = larger_score(n, parts)
            if pending is not None:
                place(*pending)
            pending = (n, parts, y)
        place(*pending)
